import numpy as np
CORES = [7,39,87,119,135,167,215,247,263,295,343,375,391,423,471,503]
N = 16
F = 128
LR = 0.5
def setup_inputs(rng):
    return {"w": rng.standard_normal((N, 128, F), dtype=np.float32) * (0.5 + np.abs(rng.standard_normal((N, 128, 1), dtype=np.float32))), "u": rng.standard_normal((N, 128, F), dtype=np.float32) * (0.5 + np.abs(rng.standard_normal((N, 128, 1), dtype=np.float32)))}
def setup_inputs_big(rng):
    d = setup_inputs(rng)
    for k in ("w", "u"): d[k] = (d[k].astype(np.float32) * 1024.0).astype(d[k].dtype)
    return d
def setup_inputs_small(rng):
    d = setup_inputs(rng)
    for k in ("w", "u"): d[k] = (d[k].astype(np.float32) * (1 / 1024.0)).astype(d[k].dtype)
    return d
def setup_inputs_apart(rng):
    d = setup_inputs(rng)
    f = (10.0 ** rng.permutation(np.linspace(-1.5, 1.5, N))).astype(np.float32).reshape(N, 1, 1)
    for k in ("w", "u"): d[k] = (d[k].astype(np.float32) * f).astype(d[k].dtype)
    return d
def setup_inputs_mixed(rng):
    d = setup_inputs(rng)
    f = (10.0 ** rng.uniform(-3, 3, (1, 128, 1))).astype(np.float32); shape = rng.integers(3, size=(1, 128, 1))
    for k in ("u",):
        x = d[k].astype(np.float32)
        m = x.mean(axis=(0, 2), keepdims=True); level = m + np.sign(x - m) * np.abs(x - m).mean(axis=(0, 2), keepdims=True) * rng.uniform(0.9, 1.1, x.shape).astype(np.float32)
        other = x * np.where(rng.random(x.shape) < 0.5, 0.1, 1.0).astype(np.float32)
        d[k] = (np.where(shape == 1, level, np.where(shape == 2, other, x)) * f).astype(d[k].dtype)
    return d
def reference(w, u):
    W, U = w.astype(np.float64), u.astype(np.float64)
    nw = np.sqrt((W ** 2).sum(axis=(0, 2)).reshape(1, 128, 1))
    nu = np.sqrt((U ** 2).sum(axis=(0, 2)).reshape(1, 128, 1))
    return {"y": (W - LR * (nw / nu) * U).astype(np.float32)}

@@ -1,0 +1,120 @@
+from concourse.bass import DstId, RemoteDMATransfer
+from concourse.mybir import AluOpType, AxisListType, ActivationFunctionType
+
+SCRATCH = {
+    "wsb": ("sbuf", [128, 128], "float32"),
+    "usb": ("sbuf", [128, 128], "float32"),
+    "sqw": ("sbuf", [128, 128], "float32"),
+    "squ": ("sbuf", [128, 128], "float32"),
+    "ug": ("sbuf", [128, 128], "float32"),
+    "ysb": ("sbuf", [128, 128], "float32"),
+    "s": ("sbuf", [128, 4], "float32"),
+    "slots": ("dram", [16, 128, 2], "float32"),
+    "land": ("sbuf", [128, 8], "float32"),
+    "sm": ("sbuf", [128, 16], "float32"),
+    "tps": ("psum", [128, 128], "float32"),
+}
+SEMAPHORES = ["ldw", "ldu", "sq", "l1", "arr1", "arr2", "sent", "e1", "e2", "e3", "e4", "e5", "e6", "e7",
+              "f1", "f2", "f3", "f4", "f5", "f6", "st"]
+
+LO, HI = 1e-16, 1e16
+RLO, RHI = 1e-8, 1e8
+
+
+def _bits(mask):
+    return [b for b in range(16) if (mask >> b) & 1]
+
+
+def rank_program(g, core, T, topo):
+    rank = T.rank_of(core)
+    if rank is None:
+        return
+    S = T.sem
+    AF, OP = ActivationFunctionType, AluOpType
+    cores = list(T.cores)
+
+    def rack(c):
+        return topo.rack(topo.host(c))
+
+    mine = sorted(d for d in cores if rack(d) == rack(core))
+    assert all(topo.same_plane(core, d) for d in mine if d != core)
+    buddy = mine[mine.index(core) ^ 1]
+    others = [d for d in mine if d != core and d != buddy]
+    partner = [d for d in cores if rack(d) != rack(core) and topo.may_write(core, d)
+               and topo.chip(d) == topo.chip(core)][0]
+
+    def dst(d):
+        rid, pid = topo.addr(d, core)
+        return DstId(rid=rid, pnc=pid)
+
+    col = lambda j: T.sm[:, j:j + 1]
+    CW, CU, RB, RR, G, G2, H, SU, REC, SWH, ROOT = range(11)
+    own = T.s[:, 0:2]
+
+    g.sync.dma_start(T.wsb[:], T.w[:]).then_inc(S.ldw, 16)
+    g.scalar.dma_start(T.usb[:], T.u[:]).then_inc(S.ldu, 16)
+    g.scalar.wait_ge(S.ldw, 16)
+    g.scalar.activation(T.sqw[:], T.wsb[:], AF.Square, accum_out=T.s[:, 0:1]).then_inc(S.sq, 1)
+    g.scalar.wait_ge(S.ldu, 16)
+    g.scalar.activation(T.squ[:], T.usb[:], AF.Square, scale=2.0, accum_out=T.s[:, 1:2]).then_inc(S.sq, 1)
+
+    g.sync.wait_ge(S.sq, 2)
+    g.sync.dma_start(T.slots[rank], own).then_inc(S.l1, 16)
+
+    g.wait_ge(S.sq, 2)
+    mb = topo.mask(core, buddy)
+    rid, pid = topo.addr(buddy, core)
+    g.remote_dma(T.slots[rank], own, S.arr1, S.sent, pid, rid, mb)
+
+    g.wait_ge(S.l1, 16)
+    calls = []
+    for i, d in enumerate(others):
+        e = _bits(topo.mask(core, d))
+        calls.append(RemoteDMATransfer(dst_ids=[dst(d)], dma_engine_mask=1 << e[i % len(e)], remote_sem=S.arr1,
+                                       src=T.slots[rank], dst=T.slots[rank]))
+    g.remote_dma_fused(calls, local_sem=S.sent)
+
+    g.wait_ge(S.arr1, len(_bits(mb)) + len(others))
+    m2 = topo.mask(core, partner) & topo.mask(core, buddy)
+    fold = RemoteDMATransfer(dst_ids=[dst(partner), dst(buddy)], dma_engine_mask=m2, remote_sem=S.arr2,
+                             srcs=[T.slots[T.rank_of(d)] for d in mine],
+                             dsts=[T.land[:, 0:2], T.land[:, 4:6]], alu_op=1)
+    g.remote_dma_fused([fold], local_sem=S.sent)
+    n2 = len(_bits(m2))
+
+    v, a = g.vector, g.scalar
+    v.wait_ge(S.sq, 2)
+    v.tensor_scalar(T.sm[:, CW:CU + 1], own, LO, HI, OP.max, OP.min).then_inc(S.e1, 1)
+    v.wait_ge(S.e1, 1)
+    v.reciprocal(col(RB), col(CU)).then_inc(S.e2, 1)
+    v.wait_ge(S.e2, 1)
+    v.tensor_scalar(col(RR), col(CW), col(RB), RHI, OP.mult, OP.min).then_inc(S.e3, 1)
+    a.wait_ge(S.e3, 1)
+    a.activation(col(G), col(RR), AF.Sqrt, bias=RLO).then_inc(S.e4, 1)
+    a.wait_ge(S.e4, 1)
+    a.activation(T.ug[:], T.usb[:], AF.Identity, scale=col(G)).then_inc(S.e7, 1)
+    v.wait_ge(S.e4, 1)
+    v.tensor_tensor(col(G2), col(G), col(G), OP.mult).then_inc(S.e5, 1)
+    v.wait_ge(S.e5, 1)
+    v.reciprocal(col(H), col(G2)).then_inc(S.e6, 1)
+
+    v.wait_ge(S.arr2, 2 * n2)
+    v.tensor_reduce(col(SU), T.land[:, 1:8:4], AxisListType.X, OP.add).then_inc(S.f1, 1)
+    v.wait_ge(S.f1, 1)
+    v.reciprocal(col(REC), col(SU)).then_inc(S.f2, 1)
+    a.wait_ge(S.arr2, 2 * n2)
+    a.wait_ge(S.e6, 1)
+    a.activation(T.sm[:, 12:14], T.land[:, 0:8:4], AF.Identity, scale=col(H), accum_out=col(SWH)).then_inc(S.f3, 1)
+    a.wait_ge(S.f3, 1)
+    a.wait_ge(S.f2, 1)
+    a.activation(col(ROOT), col(SWH), AF.Sqrt, scale=col(REC)).then_inc(S.f4, 1)
+    a.wait_ge(S.f4, 1)
+    a.wait_ge(S.e7, 1)
+    a.activation(T.tps[:], T.ug[:], AF.Identity, scale=col(ROOT)).then_inc(S.f5, 1)
+    v.wait_ge(S.f5, 1)
+    v.wait_ge(S.ldw, 16)
+    v.tensor_tensor(T.ysb[:], T.wsb[:], T.tps[:], OP.subtract).then_inc(S.f6, 1)
+    g.sync.wait_ge(S.f6, 1)
+    g.sync.dma_start(T.y[:], T.ysb[:]).then_inc(S.st, 16)
+    g.sync.wait_ge(S.st, 16)
+    g.wait_ge(S.sent, len(_bits(mb)) + len(others) + n2)

@@ -9,13 +9,13 @@ SCRATCH = {
     "ug": ("sbuf", [128, 128], "float32"),
     "ysb": ("sbuf", [128, 128], "float32"),
     "s": ("sbuf", [128, 4], "float32"),
-    "slots": ("dram", [16, 128, 2], "float32"),
-    "land": ("sbuf", [128, 8], "float32"),
-    "sm": ("sbuf", [128, 16], "float32"),
-    "tps": ("psum", [128, 128], "float32"),
+    "fin": ("sbuf", [128, 32], "float32"),
+    "sm": ("sbuf", [128, 32], "float32"),
+    "ta": ("psum", [128, 512], "float32"),
+    "tb": ("psum", [128, 512], "float32"),
 }
-SEMAPHORES = ["ldw", "ldu", "sq", "l1", "arr1", "arr2", "sent", "e1", "e2", "e3", "e4", "e5", "e6", "e7",
-              "f1", "f2", "f3", "f4", "f5", "f6", "st"]
+SEMAPHORES = ["ldw", "ldu", "sq", "cp", "arr1", "arr2", "sent", "e1", "e2", "e3", "e4", "e5", "e6", "e7",
+              "f1", "f2", "f3", "f4", "f5a", "f5b", "f6", "st"]
 
 LO, HI = 1e-16, 1e16
 RLO, RHI = 1e-8, 1e8
@@ -25,64 +25,79 @@ def _bits(mask):
     return [b for b in range(16) if (mask >> b) & 1]
 
 
+def _grid(cores, topo):
+    chips = sorted(set(topo.chip(c) for c in cores))
+    n = len(chips) // 2
+
+    def rack(c):
+        return topo.rack(topo.host(c))
+
+    def qkey(c):
+        return (rack(c), chips.index(topo.chip(c)) // n)
+
+    def quarter(c):
+        return sorted(d for d in cores if qkey(d) == qkey(c))
+
+    def line(c):
+        return sorted(d for d in cores if chips.index(topo.chip(d)) % n == chips.index(topo.chip(c)) % n
+                      and (topo.host(d) == topo.host(c) or (rack(d) != rack(c) and topo.may_write(c, d))))
+    return quarter, line, rack
+
+
 def rank_program(g, core, T, topo):
     rank = T.rank_of(core)
     if rank is None:
         return
     S = T.sem
     AF, OP = ActivationFunctionType, AluOpType
-    cores = list(T.cores)
-
-    def rack(c):
-        return topo.rack(topo.host(c))
-
-    mine = sorted(d for d in cores if rack(d) == rack(core))
-    assert all(topo.same_plane(core, d) for d in mine if d != core)
-    buddy = mine[mine.index(core) ^ 1]
-    others = [d for d in mine if d != core and d != buddy]
-    partner = [d for d in cores if rack(d) != rack(core) and topo.may_write(core, d)
-               and topo.chip(d) == topo.chip(core)][0]
+    quarter, line, rack = _grid(list(T.cores), topo)
+    q = quarter(core)
+    peers1 = [d for d in q if d != core]
+    peers2 = sorted((d for d in line(core) if d != core),
+                    key=lambda d: (-(rack(d) != rack(core)) - (topo.chip(d) != topo.chip(core)), rack(d) == rack(core)))
+    assert all(topo.same_plane(core, d) for d in peers1) and len(q) == 4 and len(peers2) == 3
 
     def dst(d):
         rid, pid = topo.addr(d, core)
         return DstId(rid=rid, pnc=pid)
 
+    def common(ds):
+        m = topo.mask(core, ds[0])
+        for d in ds:
+            m &= topo.mask(core, d)
+        return m
+
     col = lambda j: T.sm[:, j:j + 1]
     CW, CU, RB, RR, G, G2, H, SU, REC, SWH, ROOT = range(11)
+    k = q.index(core)
     own = T.s[:, 0:2]
+    place = T.fin[:, 2 * k:2 * k + 2]
+    v, a = g.vector, g.scalar
+    m1, m2 = common(peers1), common(peers2)
+    all1, all2 = len(_bits(m1)) * len(peers1), len(_bits(m2)) * len(peers2)
 
     g.sync.dma_start(T.wsb[:], T.w[:]).then_inc(S.ldw, 16)
-    g.scalar.dma_start(T.usb[:], T.u[:]).then_inc(S.ldu, 16)
-    g.scalar.wait_ge(S.ldw, 16)
-    g.scalar.activation(T.sqw[:], T.wsb[:], AF.Square, accum_out=T.s[:, 0:1]).then_inc(S.sq, 1)
-    g.scalar.wait_ge(S.ldu, 16)
-    g.scalar.activation(T.squ[:], T.usb[:], AF.Square, scale=2.0, accum_out=T.s[:, 1:2]).then_inc(S.sq, 1)
-
-    g.sync.wait_ge(S.sq, 2)
-    g.sync.dma_start(T.slots[rank], own).then_inc(S.l1, 16)
+    a.dma_start(T.usb[:], T.u[:]).then_inc(S.ldu, 16)
+    a.wait_ge(S.ldw, 16)
+    a.activation(T.sqw[:], T.wsb[:], AF.Square, accum_out=T.s[:, 0:1]).then_inc(S.sq, 1)
+    a.wait_ge(S.ldu, 16)
+    a.activation(T.squ[:], T.usb[:], AF.Square, scale=2.0, accum_out=T.s[:, 1:2]).then_inc(S.sq, 1)
 
     g.wait_ge(S.sq, 2)
-    mb = topo.mask(core, buddy)
-    rid, pid = topo.addr(buddy, core)
-    g.remote_dma(T.slots[rank], own, S.arr1, S.sent, pid, rid, mb)
+    g.remote_dma_fused([RemoteDMATransfer(dst_ids=[dst(d) for d in peers1], dma_engine_mask=m1, remote_sem=S.arr1,
+                                          srcs=[own], dsts=[place for d in peers1], alu_op=0)], local_sem=S.sent)
+    g.sync.wait_ge(S.sq, 2)
+    g.sync.dma_start(place, own).then_inc(S.cp, 16)
 
-    g.wait_ge(S.l1, 16)
-    calls = []
-    for i, d in enumerate(others):
-        e = _bits(topo.mask(core, d))
-        calls.append(RemoteDMATransfer(dst_ids=[dst(d)], dma_engine_mask=1 << e[i % len(e)], remote_sem=S.arr1,
-                                       src=T.slots[rank], dst=T.slots[rank]))
-    g.remote_dma_fused(calls, local_sem=S.sent)
+    g.wait_ge(S.arr1, all1)
+    g.wait_ge(S.cp, 16)
+    where = []
+    for d in peers2:
+        i = [e for e in line(d) if e != d].index(core)
+        where.append(T.fin[:, 8 + 8 * i:16 + 8 * i])
+    g.remote_dma_fused([RemoteDMATransfer(dst_ids=[dst(d) for d in peers2], dma_engine_mask=m2, remote_sem=S.arr2,
+                                          srcs=[T.fin[:, 0:8]], dsts=where, alu_op=0)], local_sem=S.sent)
 
-    g.wait_ge(S.arr1, len(_bits(mb)) + len(others))
-    m2 = topo.mask(core, partner) & topo.mask(core, buddy)
-    fold = RemoteDMATransfer(dst_ids=[dst(partner), dst(buddy)], dma_engine_mask=m2, remote_sem=S.arr2,
-                             srcs=[T.slots[T.rank_of(d)] for d in mine],
-                             dsts=[T.land[:, 0:2], T.land[:, 4:6]], alu_op=1)
-    g.remote_dma_fused([fold], local_sem=S.sent)
-    n2 = len(_bits(m2))
-
-    v, a = g.vector, g.scalar
     v.wait_ge(S.sq, 2)
     v.tensor_scalar(T.sm[:, CW:CU + 1], own, LO, HI, OP.max, OP.min).then_inc(S.e1, 1)
     v.wait_ge(S.e1, 1)
@@ -98,23 +113,32 @@ def rank_program(g, core, T, topo):
     v.wait_ge(S.e5, 1)
     v.reciprocal(col(H), col(G2)).then_inc(S.e6, 1)
 
-    v.wait_ge(S.arr2, 2 * n2)
-    v.tensor_reduce(col(SU), T.land[:, 1:8:4], AxisListType.X, OP.add).then_inc(S.f1, 1)
+    v.wait_ge(S.arr1, all1)
+    v.wait_ge(S.cp, 16)
+    v.wait_ge(S.arr2, all2)
+    v.tensor_reduce(col(SU), T.fin[:, 1:32:2], AxisListType.X, OP.add).then_inc(S.f1, 1)
     v.wait_ge(S.f1, 1)
     v.reciprocal(col(REC), col(SU)).then_inc(S.f2, 1)
-    a.wait_ge(S.arr2, 2 * n2)
+    a.wait_ge(S.arr1, all1)
+    a.wait_ge(S.cp, 16)
+    a.wait_ge(S.arr2, all2)
     a.wait_ge(S.e6, 1)
-    a.activation(T.sm[:, 12:14], T.land[:, 0:8:4], AF.Identity, scale=col(H), accum_out=col(SWH)).then_inc(S.f3, 1)
+    a.activation(T.sm[:, 16:32], T.fin[:, 0:32:2], AF.Identity, scale=col(H), accum_out=col(SWH)).then_inc(S.f3, 1)
     a.wait_ge(S.f3, 1)
     a.wait_ge(S.f2, 1)
     a.activation(col(ROOT), col(SWH), AF.Sqrt, scale=col(REC)).then_inc(S.f4, 1)
     a.wait_ge(S.f4, 1)
     a.wait_ge(S.e7, 1)
-    a.activation(T.tps[:], T.ug[:], AF.Identity, scale=col(ROOT)).then_inc(S.f5, 1)
-    v.wait_ge(S.f5, 1)
+    a.activation(T.ta[:, 0:64], T.ug[:, 0:64], AF.Identity, scale=col(ROOT)).then_inc(S.f5a, 1)
+    v.wait_ge(S.f4, 1)
+    v.wait_ge(S.e7, 1)
     v.wait_ge(S.ldw, 16)
-    v.tensor_tensor(T.ysb[:], T.wsb[:], T.tps[:], OP.subtract).then_inc(S.f6, 1)
-    g.sync.wait_ge(S.f6, 1)
+    v.tensor_scalar(T.tb[:, 0:64], T.ug[:, 64:128], col(ROOT), None, OP.mult).then_inc(S.f5b, 1)
+    v.wait_ge(S.f5b, 1)
+    v.tensor_tensor(T.ysb[:, 64:128], T.wsb[:, 64:128], T.tb[:, 0:64], OP.subtract).then_inc(S.f6, 1)
+    v.wait_ge(S.f5a, 1)
+    v.tensor_tensor(T.ysb[:, 0:64], T.wsb[:, 0:64], T.ta[:, 0:64], OP.subtract).then_inc(S.f6, 1)
+    g.sync.wait_ge(S.f6, 2)
     g.sync.dma_start(T.y[:], T.ysb[:]).then_inc(S.st, 16)
     g.sync.wait_ge(S.st, 16)
-    g.wait_ge(S.sent, len(_bits(mb)) + len(others) + n2)
+    g.wait_ge(S.sent, len(_bits(m1)) + len(_bits(m2)))

from concourse.bass import DstId, RemoteDMATransfer
from concourse.mybir import AluOpType, AxisListType, ActivationFunctionType

SCRATCH = {
    "wsb": ("sbuf", [128, 128], "float32"),
    "usb": ("sbuf", [128, 128], "float32"),
    "sqw": ("sbuf", [128, 128], "float32"),
    "squ": ("sbuf", [128, 128], "float32"),
    "ug": ("sbuf", [128, 128], "float32"),
    "ysb": ("sbuf", [128, 128], "float32"),
    "s": ("sbuf", [128, 4], "float32"),
    "fin": ("sbuf", [128, 32], "float32"),
    "sm": ("sbuf", [128, 32], "float32"),
    "ta": ("psum", [128, 512], "float32"),
    "tb": ("psum", [128, 512], "float32"),
}
SEMAPHORES = ["ldw", "ldu", "sq", "cp", "arr1", "arr2", "sent", "e1", "e2", "e3", "e4", "e5", "e6", "e7",
              "f1", "f2", "f3", "f4", "f5a", "f5b", "f6", "st"]

LO, HI = 1e-16, 1e16
RLO, RHI = 1e-8, 1e8


def _bits(mask):
    return [b for b in range(16) if (mask >> b) & 1]


def _grid(cores, topo):
    chips = sorted(set(topo.chip(c) for c in cores))
    n = len(chips) // 2

    def rack(c):
        return topo.rack(topo.host(c))

    def qkey(c):
        return (rack(c), chips.index(topo.chip(c)) // n)

    def quarter(c):
        return sorted(d for d in cores if qkey(d) == qkey(c))

    def line(c):
        return sorted(d for d in cores if chips.index(topo.chip(d)) % n == chips.index(topo.chip(c)) % n
                      and (topo.host(d) == topo.host(c) or (rack(d) != rack(c) and topo.may_write(c, d))))
    return quarter, line, rack


def rank_program(g, core, T, topo):
    rank = T.rank_of(core)
    if rank is None:
        return
    S = T.sem
    AF, OP = ActivationFunctionType, AluOpType
    quarter, line, rack = _grid(list(T.cores), topo)
    q = quarter(core)
    peers1 = [d for d in q if d != core]
    peers2 = sorted((d for d in line(core) if d != core),
                    key=lambda d: (-(rack(d) != rack(core)) - (topo.chip(d) != topo.chip(core)), rack(d) == rack(core)))
    assert all(topo.same_plane(core, d) for d in peers1) and len(q) == 4 and len(peers2) == 3

    def dst(d):
        rid, pid = topo.addr(d, core)
        return DstId(rid=rid, pnc=pid)

    def common(ds):
        m = topo.mask(core, ds[0])
        for d in ds:
            m &= topo.mask(core, d)
        return m

    col = lambda j: T.sm[:, j:j + 1]
    CW, CU, RB, RR, G, G2, H, SU, REC, SWH, ROOT = range(11)
    k = q.index(core)
    own = T.s[:, 0:2]
    place = T.fin[:, 2 * k:2 * k + 2]
    v, a = g.vector, g.scalar
    m1, m2 = common(peers1), common(peers2)
    all1, all2 = len(_bits(m1)) * len(peers1), len(_bits(m2)) * len(peers2)

    g.sync.dma_start(T.wsb[:], T.w[:]).then_inc(S.ldw, 16)
    a.dma_start(T.usb[:], T.u[:]).then_inc(S.ldu, 16)
    a.wait_ge(S.ldw, 16)
    a.activation(T.sqw[:], T.wsb[:], AF.Square, accum_out=T.s[:, 0:1]).then_inc(S.sq, 1)
    a.wait_ge(S.ldu, 16)
    a.activation(T.squ[:], T.usb[:], AF.Square, scale=2.0, accum_out=T.s[:, 1:2]).then_inc(S.sq, 1)

    g.wait_ge(S.sq, 2)
    g.remote_dma_fused([RemoteDMATransfer(dst_ids=[dst(d) for d in peers1], dma_engine_mask=m1, remote_sem=S.arr1,
                                          srcs=[own], dsts=[place for d in peers1], alu_op=0)], local_sem=S.sent)
    g.sync.wait_ge(S.sq, 2)
    g.sync.dma_start(place, own).then_inc(S.cp, 16)

    g.wait_ge(S.arr1, all1)
    g.wait_ge(S.cp, 16)
    where = []
    for d in peers2:
        i = [e for e in line(d) if e != d].index(core)
        where.append(T.fin[:, 8 + 8 * i:16 + 8 * i])
    g.remote_dma_fused([RemoteDMATransfer(dst_ids=[dst(d) for d in peers2], dma_engine_mask=m2, remote_sem=S.arr2,
                                          srcs=[T.fin[:, 0:8]], dsts=where, alu_op=0)], local_sem=S.sent)

    v.wait_ge(S.sq, 2)
    v.tensor_scalar(T.sm[:, CW:CU + 1], own, LO, HI, OP.max, OP.min).then_inc(S.e1, 1)
    v.wait_ge(S.e1, 1)
    v.reciprocal(col(RB), col(CU)).then_inc(S.e2, 1)
    v.wait_ge(S.e2, 1)
    v.tensor_scalar(col(RR), col(CW), col(RB), RHI, OP.mult, OP.min).then_inc(S.e3, 1)
    a.wait_ge(S.e3, 1)
    a.activation(col(G), col(RR), AF.Sqrt, bias=RLO).then_inc(S.e4, 1)
    a.wait_ge(S.e4, 1)
    a.activation(T.ug[:], T.usb[:], AF.Identity, scale=col(G)).then_inc(S.e7, 1)
    v.wait_ge(S.e4, 1)
    v.tensor_tensor(col(G2), col(G), col(G), OP.mult).then_inc(S.e5, 1)
    v.wait_ge(S.e5, 1)
    v.reciprocal(col(H), col(G2)).then_inc(S.e6, 1)

    v.wait_ge(S.arr1, all1)
    v.wait_ge(S.cp, 16)
    v.wait_ge(S.arr2, all2)
    v.tensor_reduce(col(SU), T.fin[:, 1:32:2], AxisListType.X, OP.add).then_inc(S.f1, 1)
    v.wait_ge(S.f1, 1)
    v.reciprocal(col(REC), col(SU)).then_inc(S.f2, 1)
    a.wait_ge(S.arr1, all1)
    a.wait_ge(S.cp, 16)
    a.wait_ge(S.arr2, all2)
    a.wait_ge(S.e6, 1)
    a.activation(T.sm[:, 16:32], T.fin[:, 0:32:2], AF.Identity, scale=col(H), accum_out=col(SWH)).then_inc(S.f3, 1)
    a.wait_ge(S.f3, 1)
    a.wait_ge(S.f2, 1)
    a.activation(col(ROOT), col(SWH), AF.Sqrt, scale=col(REC)).then_inc(S.f4, 1)
    a.wait_ge(S.f4, 1)
    a.wait_ge(S.e7, 1)
    a.activation(T.ta[:, 0:64], T.ug[:, 0:64], AF.Identity, scale=col(ROOT)).then_inc(S.f5a, 1)
    v.wait_ge(S.f4, 1)
    v.wait_ge(S.e7, 1)
    v.wait_ge(S.ldw, 16)
    v.tensor_scalar(T.tb[:, 0:64], T.ug[:, 64:128], col(ROOT), None, OP.mult).then_inc(S.f5b, 1)
    v.wait_ge(S.f5b, 1)
    v.tensor_tensor(T.ysb[:, 64:128], T.wsb[:, 64:128], T.tb[:, 0:64], OP.subtract).then_inc(S.f6, 1)
    v.wait_ge(S.f5a, 1)
    v.tensor_tensor(T.ysb[:, 0:64], T.wsb[:, 0:64], T.ta[:, 0:64], OP.subtract).then_inc(S.f6, 1)
    g.sync.wait_ge(S.f6, 2)
    g.sync.dma_start(T.y[:], T.ysb[:]).then_inc(S.st, 16)
    g.sync.wait_ge(S.st, 16)
    g.wait_ge(S.sent, len(_bits(m1)) + len(_bits(m2)))
